import numpy as np
import ml_dtypes


def mxq(x, axis, fmt="e4m3"):
    dtype, down = {"e4m3": (ml_dtypes.float8_e4m3fn, 7), "e5m2": (ml_dtypes.float8_e5m2, 14)}[fmt]
    v = np.moveaxis(np.asarray(x, np.float32).astype(ml_dtypes.bfloat16).astype(np.float64), axis, -1)
    blocks = v.reshape(v.shape[:-1] + (-1, 32))
    amax = np.abs(blocks).max(-1, keepdims=True)
    byte = np.maximum(np.where(amax > 0, np.frexp(amax)[1] - 1 + 127, 0) - down, 1)
    scale = np.exp2(byte - 127.0)
    codes = (blocks / scale).astype(np.float32).astype(dtype).astype(np.float64)
    return np.moveaxis((codes * scale).reshape(v.shape), -1, axis)


WIDE = False


def mx_kscale(k):
    if not WIDE:
        return np.ones(k)
    levels = np.array([10, -10, 5, -5, 0])
    if k % 512:
        return np.exp2(np.random.permutation(np.resize(levels, k // 32))).repeat(32)
    a = np.empty((k // 512, 16))
    for p in range(k // 512):
        a[p, :8] = np.random.permutation(np.resize(levels, 8))
        for g in range(8):
            far = levels[np.abs(levels - a[p, g]) >= 10]
            a[p, g + 8] = far[np.random.randint(len(far))]
    return np.exp2(a.ravel()).repeat(32)


def f64(x):
    return np.asarray(x).astype(np.float64)


def striped(idx):
    return np.tile(idx.reshape(-1, 16).T, (8, 1)).astype(np.uint16)


def unstriped(offs):
    return offs[:16].T.reshape(-1).astype(np.int64)


def pack_weight(w):
    k, n = w.shape
    w = f64(np.asarray(w, np.float32).astype(ml_dtypes.bfloat16)).reshape(k // 32, 32, n)
    amax = np.abs(w).max(1)
    byte = np.clip(np.where(amax > 0, np.frexp(amax)[1] - 1 + 127 - 7, 1), 1, 254)
    scaled = (w * np.exp2(127.0 - byte)[:, None, :]).reshape(k, n).astype(np.float32)
    words = np.ascontiguousarray(scaled.reshape(k // 512, 128, 4, n).transpose(0, 1, 3, 2)).astype(ml_dtypes.float8_e4m3fn).view(np.uint8)
    return words, np.ascontiguousarray(byte.astype(np.uint8).reshape(k // 512, 16, n))


def unpack_weight(words, scales):
    g, p, n, _ = words.shape
    vals = np.ascontiguousarray(words).view(ml_dtypes.float8_e4m3fn).astype(np.float64) * np.repeat(np.exp2(scales.astype(np.float64) - 127.0), 8, axis=1)[..., None]
    return vals.transpose(0, 1, 3, 2).reshape(g * 512, n)


K, T, S, V = 512, 1024, 512, 512
P = 2 ** 7


def setup_inputs():
    n = np.random.standard_normal
    s = mx_kscale(K)[:, None]
    packed_xT = pack_weight(n((K, T)) * s)
    packed_eT = pack_weight(n((K, T)) * s)
    return {
        "x_words": packed_xT[0],
        "x_scales": packed_xT[1],
        "e_words": packed_eT[0],
        "e_scales": packed_eT[1],
        "hr": (n((K, V)) / np.sqrt(K) / s).astype(np.float32),
        "hi": (n((K, V)) / np.sqrt(K) / s).astype(np.float32),
        "inv": (np.tile(np.random.uniform(0.5, 1.5, T), (P, 1))).astype(np.float32),
        "offs": striped(np.random.permutation(T)[:S]),
    }


def reference(x_words, x_scales, e_words, e_scales, hr, hi, inv, offs):
    hrq = mxq(f64(hr), 0, "e4m3")
    xq = unpack_weight(x_words, x_scales)[:, unstriped(offs)]
    hiq = mxq(f64(hi), 0, "e4m3")
    e_offs = unpack_weight(e_words, e_scales)[:, unstriped(offs)]
    re = hrq.T @ xq + hiq.T @ e_offs
    z = hrq.T @ e_offs
    im = (hiq.T @ xq) - z
    mm = ((re) ** 2 + (im) ** 2) * (f64(inv)[:1][:, unstriped(offs)])
    top = mm.max(axis=1, keepdims=True)
    rr = 6.0 * (mm / top)
    ex = np.exp(rr - rr.max(axis=1, keepdims=True))
    return ex / ex.sum(axis=1, keepdims=True)

@@ -1,0 +1,208 @@
+from contextlib import ExitStack
+
+import concourse.mybir as mybir
+from concourse.masks import make_identity
+
+K, T, S, V = 512, 1024, 512, 512
+FLOPS = 4 * 2 * K * S * V
+BYTES = 2 * K * T + 2 * (K // 32) * T + 2 * K * V * 4 + T * 4 + 128 * (S // 16) * 2 + V * S * 4
+
+F32 = mybir.dt.float32
+BF16 = mybir.dt.bfloat16
+I32 = mybir.dt.int32
+U32 = mybir.dt.uint32
+U16 = mybir.dt.uint16
+U8 = mybir.dt.uint8
+FP8X4 = mybir.dt.float8_e4m3fn_x4
+ALU = mybir.AluOpType
+ACT = mybir.ActivationFunctionType
+
+P = 128
+PACK = 4
+HALF = 256
+N_HALVES = V // HALF
+N_ATOM_TILES = S // P
+SHARPNESS = 6.0
+
+
+def tile_picked_ymrf_soft_p_kernel(
+    tc, x_words, x_scales, e_words, e_scales, hr, hi, inv, offs, out
+):
+    nc = tc.nc
+    with ExitStack() as ctx:
+        keep = ctx.enter_context(tc.tile_pool(name="keep", bufs=1))
+        psum = ctx.enter_context(tc.psum_pool(name="psum", bufs=1))
+
+        def bank(number, name):
+            return psum.tile([P, 512], F32, name=name, tag="bank%d" % number)
+
+        offsets = keep.tile([P, S // 16], U16, name="offsets")
+        xw_table = keep.tile([P, T], I32, name="xw_table", align_bytes=64)
+        ew_table = keep.tile([P, T], I32, name="ew_table", align_bytes=64)
+        xs_table = keep.tile([P, T], U8, name="xs_table", align_bytes=64)
+        es_table = keep.tile([P, T], U8, name="es_table", align_bytes=64)
+        inv_table = keep.tile([P, T], F32, name="inv_table", align_bytes=64)
+        identity = keep.tile([P, P], F32, name="identity", align_bytes=64)
+        shift = keep.tile([P, 1], F32, name="shift")
+        one_half = keep.tile([P, N_ATOM_TILES], F32, name="one_half")
+        warm = keep.tile([P, 1], F32, name="warm")
+
+        nc.vector.memset(shift[:], -SHARPNESS)
+        nc.vector.memset(inv_table[32:64, :], 0.0)
+        nc.vector.memset(inv_table[64:128, :], 0.0)
+        nc.scalar.activation(out=warm[:], in_=shift[:], func=ACT.Exp)
+        make_identity(nc, identity[:])
+        nc.gpsimd.memset(one_half[:], 0.5)
+
+        def load_words(table, words):
+            nc.sync.dma_start(out=table[:], in_=words[0].rearrange("p n t -> p (n t)").bitcast(I32))
+
+        def load_scales(table, scales):
+            for q in range(4):
+                nc.sync.dma_start(
+                    out=table[32 * q : 32 * q + 32, :].bitcast(I32),
+                    in_=scales[0, 4 * q : 4 * q + 4, :].rearrange("r c -> (r c)").bitcast(I32).partition_broadcast(8),
+                )
+
+        def load_signal(signal, half, name):
+            raw = keep.tile([P, PACK, HALF], F32, name=name, align_bytes=64)
+            rows = signal[:, half * HALF : (half + 1) * HALF]
+            nc.sync.dma_start(out=raw[:], in_=rows.rearrange("(p j) w -> p j w", j=PACK))
+            return raw
+
+        nc.sync.dma_start(offsets[:], offs)
+        nc.sync.dma_start(out=inv_table[0:32, :], in_=inv[0:32, :])
+        load_words(xw_table, x_words)
+        load_scales(xs_table, x_scales)
+        hr_raw = [load_signal(hr, 0, "hr_raw0")]
+        hi_raw = [load_signal(hi, 0, "hi_raw0")]
+        load_scales(es_table, e_scales)
+        load_words(ew_table, e_words)
+        hr_raw.append(load_signal(hr, 1, "hr_raw1"))
+        hi_raw.append(load_signal(hi, 1, "hi_raw1"))
+
+        xw = keep.tile([P, S], U32, name="xw", align_bytes=64)
+        ew = keep.tile([P, S], U32, name="ew", align_bytes=64)
+        xs = keep.tile([P, S], U8, name="xs", align_bytes=64)
+        es = keep.tile([P, S], U8, name="es", align_bytes=64)
+        inv_picked = keep.tile([P, S], F32, name="inv_picked", align_bytes=64)
+
+        def interleave(copy, raw, name):
+            rounded = keep.tile([P, HALF * PACK], BF16, name=name, align_bytes=64)
+            copy(
+                out=rounded[:].rearrange("p (c i j) -> p c j i", i=4, j=PACK),
+                in_=raw[:].rearrange("p j (c i) -> p c j i", i=4),
+            )
+            return rounded
+
+        def quantize(half, hr_rounded, hi_rounded):
+            codes = keep.tile([P, 3 * HALF], U32, name="codes%d" % half, align_bytes=64)
+            scales = keep.tile([P, 3 * HALF], U8, name="scales%d" % half, align_bytes=64)
+            negated = keep.tile([P, HALF * PACK], BF16, name="negated%d" % half, align_bytes=64)
+            nc.vector.tensor_scalar(out=negated[:], in0=hr_rounded[:], scalar1=-1.0, scalar2=None, op0=ALU.mult)
+            for slot, rounded in ((0, hr_rounded), (2, negated), (1, hi_rounded)):
+                cols = slice(slot * HALF, (slot + 1) * HALF)
+                nc.vector.quantize_mx(out=codes[:, cols].bitcast(FP8X4), scales=scales[:, cols], in_=rounded[:])
+            return codes, scales
+
+        def product(acc, words, word_scales, atoms, signals, first_col, first):
+            codes, scales = signals
+            cols = slice(first_col, first_col + 2 * HALF)
+            nc.tensor.matmul_mx(
+                out=acc[:],
+                lhsT=words[:, atoms].bitcast(FP8X4),
+                lhsT_scale=word_scales[:, atoms],
+                rhs=codes[:, cols].bitcast(FP8X4),
+                rhs_scale=scales[:, cols],
+                start=first,
+                stop=not first,
+            )
+
+        atom_cols = [slice(a * P, (a + 1) * P) for a in range(N_ATOM_TILES)]
+
+        nc.vector.tensor_copy(out=inv_picked[:], in_=inv_table[:].indirect(offsets[:]))
+        inv_turned = bank(7, "inv_turned")
+        for atoms in atom_cols:
+            nc.tensor.transpose(inv_turned[:, atoms], inv_picked[:, atoms], identity[:])
+        inv_column = keep.tile([P, N_ATOM_TILES], F32, name="inv_column")
+        root_inv = keep.tile([P, N_ATOM_TILES], F32, name="root_inv")
+        nc.vector.tensor_copy(out=xw[:], in_=xw_table[:].bitcast(U32).indirect(offsets[:]))
+        nc.vector.tensor_copy(out=inv_column[:], in_=inv_turned[:, 0 : S : P])
+        nc.gpsimd.tensor_tensor(out=root_inv[:], in0=inv_column[:], in1=one_half[:], op=ALU.pow)
+        nc.vector.tensor_copy(out=xs[:], in_=xs_table[:].indirect(offsets[:]))
+        hr_rounded = [interleave(nc.scalar.copy, hr_raw[0], "hr_rounded0")]
+        hi_rounded = [interleave(nc.scalar.copy, hi_raw[0], "hi_rounded0")]
+        nc.vector.tensor_copy(out=es[:], in_=es_table[:].indirect(offsets[:]))
+        signals = [quantize(0, hr_rounded[0], hi_rounded[0])]
+
+        for piece in range(2):
+            nc.vector.tensor_copy(
+                out=ew[:, piece * 256 : (piece + 1) * 256],
+                in_=ew_table[:].bitcast(U32).indirect(offsets[:, piece * 16 : (piece + 1) * 16]),
+            )
+        hr_rounded.append(interleave(nc.scalar.copy, hr_raw[1], "hr_rounded1"))
+        hi_rounded.append(interleave(nc.vector.tensor_copy, hi_raw[1], "hi_rounded1"))
+        signals.append(quantize(1, hr_rounded[1], hi_rounded[1]))
+
+        product_banks = ((0, 1, 2, 3), (6, 7, 0, 1))
+        match_banks = ((4, 5), (2, 3))
+
+        def square(half, a, acc):
+            squares = keep.tile([P, 2 * HALF], F32, name="squares%d_%d" % (half, a), align_bytes=64)
+            nc.scalar.activation(out=squares[:], in_=acc[:], func=ACT.Square, scale=root_inv[:, a : a + 1])
+            return squares
+
+        def turn(match, a, squares):
+            for s in range(2):
+                for part in range(2):
+                    first_col = part * HALF + s * P
+                    nc.tensor.matmul(
+                        match[s][:, atom_cols[a]],
+                        lhsT=squares[:, first_col : first_col + P],
+                        rhs=identity[:],
+                        is_transpose=True,
+                        start=part == 0,
+                        stop=part == 1,
+                    )
+
+        def softmax(tile_no, match):
+            scratch = keep.tile([P, S], BF16, name="scratch", tag="scratch")
+            top = keep.tile([P, 1], F32, name="top%d" % tile_no)
+            slope = keep.tile([P, 1], F32, name="slope%d" % tile_no)
+            total = keep.tile([P, 1], F32, name="total%d" % tile_no)
+            norm = keep.tile([P, 1], F32, name="norm%d" % tile_no)
+            weights = keep.tile([P, S], F32, name="weights%d" % tile_no)
+            result = keep.tile([P, S], F32, name="result%d" % tile_no)
+            nc.vector.tensor_scalar(
+                out=scratch[:], in0=match[:], scalar1=1.0 / SHARPNESS, scalar2=None,
+                op0=ALU.mult, op1=ALU.max, accum_out=top[:],
+            )
+            nc.vector.reciprocal(out=slope[:], in_=top[:])
+            nc.scalar.activation(
+                out=weights[:], in_=match[:], func=ACT.Exp, bias=shift[:], scale=slope[:], accum_out=total[:]
+            )
+            nc.vector.reciprocal(out=norm[:], in_=total[:])
+            nc.vector.tensor_scalar(out=result[:], in0=weights[:], scalar1=norm[:], scalar2=None, op0=ALU.mult)
+            nc.sync.dma_start(out=out[tile_no * P : (tile_no + 1) * P, :], in_=result[:])
+
+        accs = [bank(b, "acc0_%d" % a) for a, b in enumerate(product_banks[0])]
+        for a in range(N_ATOM_TILES):
+            product(accs[a], xw, xs, atom_cols[a], signals[0], 0, True)
+        for a in range(N_ATOM_TILES):
+            product(accs[a], ew, es, atom_cols[a], signals[0], HALF, False)
+        squares0 = [square(0, a, accs[a]) for a in range(N_ATOM_TILES)]
+
+        match0 = [bank(b, "match0_%d" % s) for s, b in enumerate(match_banks[0])]
+        squares1 = []
+        for a in range(N_ATOM_TILES):
+            acc = bank(product_banks[1][a], "acc1_%d" % a)
+            product(acc, xw, xs, atom_cols[a], signals[1], 0, True)
+            product(acc, ew, es, atom_cols[a], signals[1], HALF, False)
+            squares1.append(square(1, a, acc))
+            turn(match0, a, squares0[a])
+        match1 = [bank(b, "match1_%d" % s) for s, b in enumerate(match_banks[1])]
+        for a in range(N_ATOM_TILES):
+            turn(match1, a, squares1[a])
+        for half, match in enumerate((match0, match1)):
+            for s in range(2):
+                softmax(2 * half + s, match[s])

@@ -46,6 +46,7 @@ def tile_picked_ymrf_soft_p_kernel(
         shift = keep.tile([P, 1], F32, name="shift")
         one_half = keep.tile([P, N_ATOM_TILES], F32, name="one_half")
         warm = keep.tile([P, 1], F32, name="warm")
+        minus_one = keep.tile([P, 1], F32, name="minus_one")
 
         nc.vector.memset(shift[:], -SHARPNESS)
         nc.vector.memset(inv_table[32:64, :], 0.0)
@@ -53,6 +54,7 @@ def tile_picked_ymrf_soft_p_kernel(
         nc.scalar.activation(out=warm[:], in_=shift[:], func=ACT.Exp)
         make_identity(nc, identity[:])
         nc.gpsimd.memset(one_half[:], 0.5)
+        nc.gpsimd.memset(minus_one[:], -1.0)
 
         def load_words(table, words):
             nc.sync.dma_start(out=table[:], in_=words[0].rearrange("p n t -> p (n t)").bitcast(I32))
@@ -65,16 +67,16 @@ def tile_picked_ymrf_soft_p_kernel(
                 )
 
         def load_signal(signal, half, name):
-            raw = keep.tile([P, PACK, HALF], F32, name=name, align_bytes=64)
+            raw = keep.tile([P, PACK, HALF], F32, name=name, tag=name, align_bytes=64)
             rows = signal[:, half * HALF : (half + 1) * HALF]
             nc.sync.dma_start(out=raw[:], in_=rows.rearrange("(p j) w -> p j w", j=PACK))
             return raw
 
         nc.sync.dma_start(offsets[:], offs)
         nc.sync.dma_start(out=inv_table[0:32, :], in_=inv[0:32, :])
-        load_words(xw_table, x_words)
         load_scales(xs_table, x_scales)
         hr_raw = [load_signal(hr, 0, "hr_raw0")]
+        load_words(xw_table, x_words)
         hi_raw = [load_signal(hi, 0, "hi_raw0")]
         load_scales(es_table, e_scales)
         load_words(ew_table, e_words)
@@ -87,20 +89,21 @@ def tile_picked_ymrf_soft_p_kernel(
         es = keep.tile([P, S], U8, name="es", align_bytes=64)
         inv_picked = keep.tile([P, S], F32, name="inv_picked", align_bytes=64)
 
-        def interleave(copy, raw, name):
-            rounded = keep.tile([P, HALF * PACK], BF16, name=name, align_bytes=64)
+        def interleave(copy, raw, name, tag=None):
+            rounded = keep.tile([P, HALF * PACK], BF16, name=name, tag=tag or name, align_bytes=64)
             copy(
                 out=rounded[:].rearrange("p (c i j) -> p c j i", i=4, j=PACK),
                 in_=raw[:].rearrange("p j (c i) -> p c j i", i=4),
             )
             return rounded
 
-        def quantize(half, hr_rounded, hi_rounded):
+        def negating_copy(out, in_):
+            nc.scalar.activation(out=out, in_=in_, func=ACT.Copy, scale=-1.0)
+
+        def quantize(half, hr_rounded, hi_rounded, negated):
             codes = keep.tile([P, 3 * HALF], U32, name="codes%d" % half, align_bytes=64)
             scales = keep.tile([P, 3 * HALF], U8, name="scales%d" % half, align_bytes=64)
-            negated = keep.tile([P, HALF * PACK], BF16, name="negated%d" % half, align_bytes=64)
-            nc.vector.tensor_scalar(out=negated[:], in0=hr_rounded[:], scalar1=-1.0, scalar2=None, op0=ALU.mult)
-            for slot, rounded in ((0, hr_rounded), (2, negated), (1, hi_rounded)):
+            for slot, rounded in enumerate((hr_rounded, hi_rounded, negated)):
                 cols = slice(slot * HALF, (slot + 1) * HALF)
                 nc.vector.quantize_mx(out=codes[:, cols].bitcast(FP8X4), scales=scales[:, cols], in_=rounded[:])
             return codes, scales
@@ -125,30 +128,43 @@ def tile_picked_ymrf_soft_p_kernel(
         for atoms in atom_cols:
             nc.tensor.transpose(inv_turned[:, atoms], inv_picked[:, atoms], identity[:])
         inv_column = keep.tile([P, N_ATOM_TILES], F32, name="inv_column")
-        root_inv = keep.tile([P, N_ATOM_TILES], F32, name="root_inv")
-        nc.vector.tensor_copy(out=xw[:], in_=xw_table[:].bitcast(U32).indirect(offsets[:]))
+        root_inv = keep.tile([P, N_ATOM_TILES], F32, name="root_inv", tag="after_squares")
+        nc.vector.tensor_copy(out=xs[:], in_=xs_table[:].indirect(offsets[:]))
         nc.vector.tensor_copy(out=inv_column[:], in_=inv_turned[:, 0 : S : P])
         nc.gpsimd.tensor_tensor(out=root_inv[:], in0=inv_column[:], in1=one_half[:], op=ALU.pow)
-        nc.vector.tensor_copy(out=xs[:], in_=xs_table[:].indirect(offsets[:]))
+        nc.vector.tensor_copy(out=xw[:], in_=xw_table[:].bitcast(U32).indirect(offsets[:]))
+        def keep_warm(number, name):
+            nc.tensor.matmul_mx(
+                out=bank(number, name)[:], lhsT=xw[:, 0:P].bitcast(FP8X4), lhsT_scale=xs[:, 0:P],
+                rhs=xw[:].bitcast(FP8X4), rhs_scale=xs[:], start=True, stop=True,
+            )
+
+        keep_warm(5, "warm0")
+        keep_warm(6, "warm1")
         hr_rounded = [interleave(nc.scalar.copy, hr_raw[0], "hr_rounded0")]
         hi_rounded = [interleave(nc.scalar.copy, hi_raw[0], "hi_rounded0")]
         nc.vector.tensor_copy(out=es[:], in_=es_table[:].indirect(offsets[:]))
-        signals = [quantize(0, hr_rounded[0], hi_rounded[0])]
+        negated = [interleave(negating_copy, hr_raw[0], "negated0")]
+        signals = [quantize(0, hr_rounded[0], hi_rounded[0], negated[0])]
 
         for piece in range(2):
             nc.vector.tensor_copy(
                 out=ew[:, piece * 256 : (piece + 1) * 256],
                 in_=ew_table[:].bitcast(U32).indirect(offsets[:, piece * 16 : (piece + 1) * 16]),
             )
-        hr_rounded.append(interleave(nc.scalar.copy, hr_raw[1], "hr_rounded1"))
-        hi_rounded.append(interleave(nc.vector.tensor_copy, hi_raw[1], "hi_rounded1"))
-        signals.append(quantize(1, hr_rounded[1], hi_rounded[1]))
+        hr_rounded.append(interleave(nc.vector.tensor_copy, hr_raw[1], "hr_rounded1", "hi_raw0"))
+        hi_rounded.append(interleave(nc.vector.tensor_copy, hi_raw[1], "hi_rounded1", "hi_rounded0"))
+        negated.append(keep.tile([P, HALF * PACK], BF16, name="negated1", align_bytes=64))
+        nc.vector.tensor_scalar(out=negated[1][:], in0=hr_rounded[1][:], scalar1=-1.0, scalar2=None, op0=ALU.mult)
+        signals.append(quantize(1, hr_rounded[1], hi_rounded[1], negated[1]))
 
         product_banks = ((0, 1, 2, 3), (6, 7, 0, 1))
         match_banks = ((4, 5), (2, 3))
 
         def square(half, a, acc):
-            squares = keep.tile([P, 2 * HALF], F32, name="squares%d_%d" % (half, a), align_bytes=64)
+            name = "squares%d_%d" % (half, a)
+            tag = name
+            squares = keep.tile([P, 2 * HALF], F32, name=name, tag=tag, align_bytes=64)
             nc.scalar.activation(out=squares[:], in_=acc[:], func=ACT.Square, scale=root_inv[:, a : a + 1])
             return squares
 
@@ -165,25 +181,39 @@ def tile_picked_ymrf_soft_p_kernel(
                         stop=part == 1,
                     )
 
-        def softmax(tile_no, match):
+        def find_slope(v, match):
             scratch = keep.tile([P, S], BF16, name="scratch", tag="scratch")
-            top = keep.tile([P, 1], F32, name="top%d" % tile_no)
-            slope = keep.tile([P, 1], F32, name="slope%d" % tile_no)
-            total = keep.tile([P, 1], F32, name="total%d" % tile_no)
-            norm = keep.tile([P, 1], F32, name="norm%d" % tile_no)
-            weights = keep.tile([P, S], F32, name="weights%d" % tile_no)
-            result = keep.tile([P, S], F32, name="result%d" % tile_no)
+            top = keep.tile([P, 1], F32, name="top%d" % v)
+            slope = keep.tile([P, 1], F32, name="slope%d" % v)
             nc.vector.tensor_scalar(
                 out=scratch[:], in0=match[:], scalar1=1.0 / SHARPNESS, scalar2=None,
                 op0=ALU.mult, op1=ALU.max, accum_out=top[:],
             )
             nc.vector.reciprocal(out=slope[:], in_=top[:])
+            return slope
+
+        def softmax(v, match, slope):
+            total = keep.tile([P, 1], F32, name="total%d" % v, tag="after_squares" if v == 0 else "total%d" % v)
+            norm = keep.tile([P, 1], F32, name="norm%d" % v)
+            weights = keep.tile([P, S], F32, name="weights%d" % v)
+            result = keep.tile([P, S], F32, name="result%d" % v)
             nc.scalar.activation(
                 out=weights[:], in_=match[:], func=ACT.Exp, bias=shift[:], scale=slope[:], accum_out=total[:]
             )
-            nc.vector.reciprocal(out=norm[:], in_=total[:])
-            nc.vector.tensor_scalar(out=result[:], in0=weights[:], scalar1=norm[:], scalar2=None, op0=ALU.mult)
-            nc.sync.dma_start(out=out[tile_no * P : (tile_no + 1) * P, :], in_=result[:])
+            if v < 2:
+                nc.gpsimd.tensor_tensor(out=norm[:], in0=total[:], in1=minus_one[:], op=ALU.pow)
+                nc.gpsimd.tensor_scalar(
+                    out=result[:], in0=weights[:], scalar1=norm[:], scalar2=0.0, op0=ALU.mult, op1=ALU.add
+                )
+            else:
+                nc.vector.reciprocal(out=norm[:], in_=total[:])
+                for cols in (slice(0, 256), slice(256, 512)) if v == 3 else (slice(0, 512),):
+                    nc.vector.tensor_scalar(
+                        out=result[:, cols], in0=weights[:, cols], scalar1=norm[:], scalar2=None, op0=ALU.mult
+                    )
+                    nc.sync.dma_start(out=out[v * P : (v + 1) * P, cols], in_=result[:, cols])
+                return
+            nc.sync.dma_start(out=out[v * P : (v + 1) * P, :], in_=result[:])
 
         accs = [bank(b, "acc0_%d" % a) for a, b in enumerate(product_banks[0])]
         for a in range(N_ATOM_TILES):
@@ -193,16 +223,20 @@ def tile_picked_ymrf_soft_p_kernel(
         squares0 = [square(0, a, accs[a]) for a in range(N_ATOM_TILES)]
 
         match0 = [bank(b, "match0_%d" % s) for s, b in enumerate(match_banks[0])]
+        for a in range(N_ATOM_TILES):
+            if a in (1, 2):
+                keep_warm(a, "warm%d" % (a + 1))
+            turn(match0, a, squares0[a])
         squares1 = []
         for a in range(N_ATOM_TILES):
             acc = bank(product_banks[1][a], "acc1_%d" % a)
             product(acc, xw, xs, atom_cols[a], signals[1], 0, True)
             product(acc, ew, es, atom_cols[a], signals[1], HALF, False)
             squares1.append(square(1, a, acc))
-            turn(match0, a, squares0[a])
+        slopes = [find_slope(s, match0[s]) for s in range(2)]
         match1 = [bank(b, "match1_%d" % s) for s, b in enumerate(match_banks[1])]
         for a in range(N_ATOM_TILES):
             turn(match1, a, squares1[a])
-        for half, match in enumerate((match0, match1)):
-            for s in range(2):
-                softmax(2 * half + s, match[s])
+        slopes.extend(find_slope(2 + s, match1[s]) for s in range(2))
+        for v, match in enumerate(match0 + match1):
+            softmax(v, match, slopes[v])

@@ -44,16 +44,17 @@ def tile_picked_ymrf_soft_p_kernel(
         inv_table = keep.tile([P, T], F32, name="inv_table", align_bytes=64)
         identity = keep.tile([P, P], F32, name="identity", align_bytes=64)
         shift = keep.tile([P, 1], F32, name="shift")
-        one_half = keep.tile([P, N_ATOM_TILES], F32, name="one_half")
-        warm = keep.tile([P, 1], F32, name="warm")
+        one = keep.tile([P, 1], F32, name="one")
+        warm_sqrt = keep.tile([P, 1], F32, name="warm_sqrt")
+        warm_exp = keep.tile([P, 1], F32, name="warm_exp")
         minus_one = keep.tile([P, 1], F32, name="minus_one")
 
         nc.vector.memset(shift[:], -SHARPNESS)
+        nc.vector.memset(one[:], 1.0)
         nc.vector.memset(inv_table[32:64, :], 0.0)
         nc.vector.memset(inv_table[64:128, :], 0.0)
-        nc.scalar.activation(out=warm[:], in_=shift[:], func=ACT.Exp)
+        nc.scalar.activation(out=warm_sqrt[:], in_=one[:], func=ACT.Sqrt)
         make_identity(nc, identity[:])
-        nc.gpsimd.memset(one_half[:], 0.5)
         nc.gpsimd.memset(minus_one[:], -1.0)
 
         def load_words(table, words):
@@ -100,13 +101,15 @@ def tile_picked_ymrf_soft_p_kernel(
         def negating_copy(out, in_):
             nc.scalar.activation(out=out, in_=in_, func=ACT.Copy, scale=-1.0)
 
-        def quantize(half, hr_rounded, hi_rounded, negated):
+        def signal_tiles(half):
             codes = keep.tile([P, 3 * HALF], U32, name="codes%d" % half, align_bytes=64)
             scales = keep.tile([P, 3 * HALF], U8, name="scales%d" % half, align_bytes=64)
-            for slot, rounded in enumerate((hr_rounded, hi_rounded, negated)):
-                cols = slice(slot * HALF, (slot + 1) * HALF)
-                nc.vector.quantize_mx(out=codes[:, cols].bitcast(FP8X4), scales=scales[:, cols], in_=rounded[:])
             return codes, scales
+
+        def quantize(signal, slot, rounded):
+            codes, scales = signal
+            cols = slice(slot * HALF, (slot + 1) * HALF)
+            nc.vector.quantize_mx(out=codes[:, cols].bitcast(FP8X4), scales=scales[:, cols], in_=rounded[:])
 
         def product(acc, words, word_scales, atoms, signals, first_col, first):
             codes, scales = signals
@@ -127,11 +130,9 @@ def tile_picked_ymrf_soft_p_kernel(
         inv_turned = bank(7, "inv_turned")
         for atoms in atom_cols:
             nc.tensor.transpose(inv_turned[:, atoms], inv_picked[:, atoms], identity[:])
-        inv_column = keep.tile([P, N_ATOM_TILES], F32, name="inv_column")
         root_inv = keep.tile([P, N_ATOM_TILES], F32, name="root_inv", tag="after_squares")
         nc.vector.tensor_copy(out=xs[:], in_=xs_table[:].indirect(offsets[:]))
-        nc.vector.tensor_copy(out=inv_column[:], in_=inv_turned[:, 0 : S : P])
-        nc.gpsimd.tensor_tensor(out=root_inv[:], in0=inv_column[:], in1=one_half[:], op=ALU.pow)
+        nc.scalar.activation(out=root_inv[:], in_=inv_turned[:, 0 : S : P], func=ACT.Sqrt)
         nc.vector.tensor_copy(out=xw[:], in_=xw_table[:].bitcast(U32).indirect(offsets[:]))
         def keep_warm(number, name):
             nc.tensor.matmul_mx(
@@ -142,10 +143,13 @@ def tile_picked_ymrf_soft_p_kernel(
         keep_warm(5, "warm0")
         keep_warm(6, "warm1")
         hr_rounded = [interleave(nc.scalar.copy, hr_raw[0], "hr_rounded0")]
-        hi_rounded = [interleave(nc.scalar.copy, hi_raw[0], "hi_rounded0")]
         nc.vector.tensor_copy(out=es[:], in_=es_table[:].indirect(offsets[:]))
         negated = [interleave(negating_copy, hr_raw[0], "negated0")]
-        signals = [quantize(0, hr_rounded[0], hi_rounded[0], negated[0])]
+        hi_rounded = [interleave(nc.scalar.copy, hi_raw[0], "hi_rounded0")]
+        signals = [signal_tiles(0)]
+        for slot, rounded in ((0, hr_rounded[0]), (2, negated[0]), (1, hi_rounded[0])):
+            quantize(signals[0], slot, rounded)
+        nc.scalar.activation(out=warm_exp[:], in_=hi_rounded[0][:, 0:1], func=ACT.Exp, scale=0.0)
 
         for piece in range(2):
             nc.vector.tensor_copy(
@@ -153,10 +157,13 @@ def tile_picked_ymrf_soft_p_kernel(
                 in_=ew_table[:].bitcast(U32).indirect(offsets[:, piece * 16 : (piece + 1) * 16]),
             )
         hr_rounded.append(interleave(nc.vector.tensor_copy, hr_raw[1], "hr_rounded1", "hi_raw0"))
-        hi_rounded.append(interleave(nc.vector.tensor_copy, hi_raw[1], "hi_rounded1", "hi_rounded0"))
         negated.append(keep.tile([P, HALF * PACK], BF16, name="negated1", align_bytes=64))
         nc.vector.tensor_scalar(out=negated[1][:], in0=hr_rounded[1][:], scalar1=-1.0, scalar2=None, op0=ALU.mult)
-        signals.append(quantize(1, hr_rounded[1], hi_rounded[1], negated[1]))
+        signals.append(signal_tiles(1))
+        quantize(signals[1], 0, hr_rounded[1])
+        quantize(signals[1], 2, negated[1])
+        hi_rounded.append(interleave(nc.vector.tensor_copy, hi_raw[1], "hi_rounded1", "hi_raw0"))
+        quantize(signals[1], 1, hi_rounded[1])
 
         product_banks = ((0, 1, 2, 3), (6, 7, 0, 1))
         match_banks = ((4, 5), (2, 3))

@@ -44,17 +44,16 @@ def tile_picked_ymrf_soft_p_kernel(
         inv_table = keep.tile([P, T], F32, name="inv_table", align_bytes=64)
         identity = keep.tile([P, P], F32, name="identity", align_bytes=64)
         shift = keep.tile([P, 1], F32, name="shift")
-        one = keep.tile([P, 1], F32, name="one")
-        warm_sqrt = keep.tile([P, 1], F32, name="warm_sqrt")
+        one_half = keep.tile([P, N_ATOM_TILES], F32, name="one_half")
         warm_exp = keep.tile([P, 1], F32, name="warm_exp")
         minus_one = keep.tile([P, 1], F32, name="minus_one")
 
         nc.vector.memset(shift[:], -SHARPNESS)
-        nc.vector.memset(one[:], 1.0)
         nc.vector.memset(inv_table[32:64, :], 0.0)
         nc.vector.memset(inv_table[64:128, :], 0.0)
-        nc.scalar.activation(out=warm_sqrt[:], in_=one[:], func=ACT.Sqrt)
+        nc.scalar.activation(out=warm_exp[:], in_=shift[:], func=ACT.Exp)
         make_identity(nc, identity[:])
+        nc.gpsimd.memset(one_half[:], 0.5)
         nc.gpsimd.memset(minus_one[:], -1.0)
 
         def load_words(table, words):
@@ -132,7 +131,9 @@ def tile_picked_ymrf_soft_p_kernel(
             nc.tensor.transpose(inv_turned[:, atoms], inv_picked[:, atoms], identity[:])
         root_inv = keep.tile([P, N_ATOM_TILES], F32, name="root_inv", tag="after_squares")
         nc.vector.tensor_copy(out=xs[:], in_=xs_table[:].indirect(offsets[:]))
-        nc.scalar.activation(out=root_inv[:], in_=inv_turned[:, 0 : S : P], func=ACT.Sqrt)
+        inv_column = keep.tile([P, N_ATOM_TILES], F32, name="inv_column")
+        nc.scalar.copy(out=inv_column[:], in_=inv_turned[:, 0 : S : P])
+        nc.gpsimd.tensor_tensor(out=root_inv[:], in0=inv_column[:], in1=one_half[:], op=ALU.pow)
         nc.vector.tensor_copy(out=xw[:], in_=xw_table[:].bitcast(U32).indirect(offsets[:]))
         def keep_warm(number, name):
             nc.tensor.matmul_mx(
@@ -149,7 +150,6 @@ def tile_picked_ymrf_soft_p_kernel(
         signals = [signal_tiles(0)]
         for slot, rounded in ((0, hr_rounded[0]), (2, negated[0]), (1, hi_rounded[0])):
             quantize(signals[0], slot, rounded)
-        nc.scalar.activation(out=warm_exp[:], in_=hi_rounded[0][:, 0:1], func=ACT.Exp, scale=0.0)
 
         for piece in range(2):
             nc.vector.tensor_copy(
@@ -188,10 +188,16 @@ def tile_picked_ymrf_soft_p_kernel(
                         stop=part == 1,
                     )
 
+        def add_and_turn(match, a, squares, engine, tag):
+            summed = keep.tile([P, HALF], F32, name="summed_" + tag, tag=tag, align_bytes=64)
+            engine.tensor_tensor(out=summed[:], in0=squares[:, 0:HALF], in1=squares[:, HALF : 2 * HALF], op=ALU.add)
+            for s in range(2):
+                nc.tensor.transpose(match[s][:, atom_cols[a]], summed[:, s * P : (s + 1) * P], identity[:])
+
         def find_slope(v, match):
             scratch = keep.tile([P, S], BF16, name="scratch", tag="scratch")
             top = keep.tile([P, 1], F32, name="top%d" % v)
-            slope = keep.tile([P, 1], F32, name="slope%d" % v)
+            slope = keep.tile([P, 1], F32, name="slope%d" % v, tag="slope%d" % v)
             nc.vector.tensor_scalar(
                 out=scratch[:], in0=match[:], scalar1=1.0 / SHARPNESS, scalar2=None,
                 op0=ALU.mult, op1=ALU.max, accum_out=top[:],
@@ -200,25 +206,32 @@ def tile_picked_ymrf_soft_p_kernel(
             return slope
 
         def softmax(v, match, slope):
-            total = keep.tile([P, 1], F32, name="total%d" % v, tag="after_squares" if v == 0 else "total%d" % v)
+            tag = ("after_squares", "slope0", "total2", "total3")[v]
+            width = N_ATOM_TILES if v == 0 else 1
+            totals = keep.tile([P, width], F32, name="total%d" % v, tag=tag)
+            total = totals[:, width - 1 : width]
             norm = keep.tile([P, 1], F32, name="norm%d" % v)
             weights = keep.tile([P, S], F32, name="weights%d" % v)
             result = keep.tile([P, S], F32, name="result%d" % v)
             nc.scalar.activation(
-                out=weights[:], in_=match[:], func=ACT.Exp, bias=shift[:], scale=slope[:], accum_out=total[:]
+                out=weights[:], in_=match[:], func=ACT.Exp, bias=shift[:], scale=slope[:], accum_out=total
             )
-            if v < 2:
-                nc.gpsimd.tensor_tensor(out=norm[:], in0=total[:], in1=minus_one[:], op=ALU.pow)
+            if v == 0:
+                nc.gpsimd.tensor_tensor(out=norm[:], in0=total, in1=minus_one[:], op=ALU.pow)
                 nc.gpsimd.tensor_scalar(
                     out=result[:], in0=weights[:], scalar1=norm[:], scalar2=0.0, op0=ALU.mult, op1=ALU.add
                 )
             else:
-                nc.vector.reciprocal(out=norm[:], in_=total[:])
-                for cols in (slice(0, 256), slice(256, 512)) if v == 3 else (slice(0, 512),):
-                    nc.vector.tensor_scalar(
-                        out=result[:, cols], in0=weights[:, cols], scalar1=norm[:], scalar2=None, op0=ALU.mult
-                    )
-                    nc.sync.dma_start(out=out[v * P : (v + 1) * P, cols], in_=result[:, cols])
+                nc.vector.reciprocal(out=norm[:], in_=total)
+                cols = slice(0, 256 if v == 3 else 512)
+                nc.vector.tensor_scalar(
+                    out=result[:, cols], in0=weights[:, cols], scalar1=norm[:], scalar2=None, op0=ALU.mult
+                )
+                nc.sync.dma_start(out=out[v * P : (v + 1) * P, cols], in_=result[:, cols])
+                if v == 3:
+                    cols = slice(256, 512)
+                    nc.scalar.activation(out=result[:, cols], in_=weights[:, cols], func=ACT.Copy, scale=norm[:])
+                    nc.scalar.dma_start(out=out[v * P : (v + 1) * P, cols], in_=result[:, cols])
                 return
             nc.sync.dma_start(out=out[v * P : (v + 1) * P, :], in_=result[:])
 
@@ -230,9 +243,9 @@ def tile_picked_ymrf_soft_p_kernel(
         squares0 = [square(0, a, accs[a]) for a in range(N_ATOM_TILES)]
 
         match0 = [bank(b, "match0_%d" % s) for s, b in enumerate(match_banks[0])]
-        for a in range(N_ATOM_TILES):
-            if a in (1, 2):
-                keep_warm(a, "warm%d" % (a + 1))
+        for a in range(N_ATOM_TILES - 1):
+            if a == 1:
+                keep_warm(a, "warm2")
             turn(match0, a, squares0[a])
         squares1 = []
         for a in range(N_ATOM_TILES):
@@ -240,10 +253,13 @@ def tile_picked_ymrf_soft_p_kernel(
             product(acc, xw, xs, atom_cols[a], signals[1], 0, True)
             product(acc, ew, es, atom_cols[a], signals[1], HALF, False)
             squares1.append(square(1, a, acc))
+            if a == 0:
+                add_and_turn(match0, 3, squares0[3], nc.vector, "hi_raw0")
         slopes = [find_slope(s, match0[s]) for s in range(2)]
         match1 = [bank(b, "match1_%d" % s) for s, b in enumerate(match_banks[1])]
-        for a in range(N_ATOM_TILES):
-            turn(match1, a, squares1[a])
+        for a in range(N_ATOM_TILES - 1):
+            add_and_turn(match1, a, squares1[a], nc.gpsimd if a == 0 else nc.vector, "sum%d" % a)
+        turn(match1, 3, squares1[3])
         slopes.extend(find_slope(2 + s, match1[s]) for s in range(2))
         for v, match in enumerate(match0 + match1):
             softmax(v, match, slopes[v])

@@ -135,14 +135,6 @@ def tile_picked_ymrf_soft_p_kernel(
         nc.scalar.copy(out=inv_column[:], in_=inv_turned[:, 0 : S : P])
         nc.gpsimd.tensor_tensor(out=root_inv[:], in0=inv_column[:], in1=one_half[:], op=ALU.pow)
         nc.vector.tensor_copy(out=xw[:], in_=xw_table[:].bitcast(U32).indirect(offsets[:]))
-        def keep_warm(number, name):
-            nc.tensor.matmul_mx(
-                out=bank(number, name)[:], lhsT=xw[:, 0:P].bitcast(FP8X4), lhsT_scale=xs[:, 0:P],
-                rhs=xw[:].bitcast(FP8X4), rhs_scale=xs[:], start=True, stop=True,
-            )
-
-        keep_warm(5, "warm0")
-        keep_warm(6, "warm1")
         hr_rounded = [interleave(nc.scalar.copy, hr_raw[0], "hr_rounded0")]
         nc.vector.tensor_copy(out=es[:], in_=es_table[:].indirect(offsets[:]))
         negated = [interleave(negating_copy, hr_raw[0], "negated0")]
@@ -244,8 +236,6 @@ def tile_picked_ymrf_soft_p_kernel(
 
         match0 = [bank(b, "match0_%d" % s) for s, b in enumerate(match_banks[0])]
         for a in range(N_ATOM_TILES - 1):
-            if a == 1:
-                keep_warm(a, "warm2")
             turn(match0, a, squares0[a])
         squares1 = []
         for a in range(N_ATOM_TILES):

from contextlib import ExitStack

import concourse.mybir as mybir
from concourse.masks import make_identity

K, T, S, V = 512, 1024, 512, 512
FLOPS = 4 * 2 * K * S * V
BYTES = 2 * K * T + 2 * (K // 32) * T + 2 * K * V * 4 + T * 4 + 128 * (S // 16) * 2 + V * S * 4

F32 = mybir.dt.float32
BF16 = mybir.dt.bfloat16
I32 = mybir.dt.int32
U32 = mybir.dt.uint32
U16 = mybir.dt.uint16
U8 = mybir.dt.uint8
FP8X4 = mybir.dt.float8_e4m3fn_x4
ALU = mybir.AluOpType
ACT = mybir.ActivationFunctionType

P = 128
PACK = 4
HALF = 256
N_HALVES = V // HALF
N_ATOM_TILES = S // P
SHARPNESS = 6.0


def tile_picked_ymrf_soft_p_kernel(
    tc, x_words, x_scales, e_words, e_scales, hr, hi, inv, offs, out
):
    nc = tc.nc
    with ExitStack() as ctx:
        keep = ctx.enter_context(tc.tile_pool(name="keep", bufs=1))
        psum = ctx.enter_context(tc.psum_pool(name="psum", bufs=1))

        def bank(number, name):
            return psum.tile([P, 512], F32, name=name, tag="bank%d" % number)

        offsets = keep.tile([P, S // 16], U16, name="offsets")
        xw_table = keep.tile([P, T], I32, name="xw_table", align_bytes=64)
        ew_table = keep.tile([P, T], I32, name="ew_table", align_bytes=64)
        xs_table = keep.tile([P, T], U8, name="xs_table", align_bytes=64)
        es_table = keep.tile([P, T], U8, name="es_table", align_bytes=64)
        inv_table = keep.tile([P, T], F32, name="inv_table", align_bytes=64)
        identity = keep.tile([P, P], F32, name="identity", align_bytes=64)
        shift = keep.tile([P, 1], F32, name="shift")
        one_half = keep.tile([P, N_ATOM_TILES], F32, name="one_half")
        warm_exp = keep.tile([P, 1], F32, name="warm_exp")
        minus_one = keep.tile([P, 1], F32, name="minus_one")

        nc.vector.memset(shift[:], -SHARPNESS)
        nc.vector.memset(inv_table[32:64, :], 0.0)
        nc.vector.memset(inv_table[64:128, :], 0.0)
        nc.scalar.activation(out=warm_exp[:], in_=shift[:], func=ACT.Exp)
        make_identity(nc, identity[:])
        nc.gpsimd.memset(one_half[:], 0.5)
        nc.gpsimd.memset(minus_one[:], -1.0)

        def load_words(table, words):
            nc.sync.dma_start(out=table[:], in_=words[0].rearrange("p n t -> p (n t)").bitcast(I32))

        def load_scales(table, scales):
            for q in range(4):
                nc.sync.dma_start(
                    out=table[32 * q : 32 * q + 32, :].bitcast(I32),
                    in_=scales[0, 4 * q : 4 * q + 4, :].rearrange("r c -> (r c)").bitcast(I32).partition_broadcast(8),
                )

        def load_signal(signal, half, name):
            raw = keep.tile([P, PACK, HALF], F32, name=name, tag=name, align_bytes=64)
            rows = signal[:, half * HALF : (half + 1) * HALF]
            nc.sync.dma_start(out=raw[:], in_=rows.rearrange("(p j) w -> p j w", j=PACK))
            return raw

        nc.sync.dma_start(offsets[:], offs)
        nc.sync.dma_start(out=inv_table[0:32, :], in_=inv[0:32, :])
        load_scales(xs_table, x_scales)
        hr_raw = [load_signal(hr, 0, "hr_raw0")]
        load_words(xw_table, x_words)
        hi_raw = [load_signal(hi, 0, "hi_raw0")]
        load_scales(es_table, e_scales)
        load_words(ew_table, e_words)
        hr_raw.append(load_signal(hr, 1, "hr_raw1"))
        hi_raw.append(load_signal(hi, 1, "hi_raw1"))

        xw = keep.tile([P, S], U32, name="xw", align_bytes=64)
        ew = keep.tile([P, S], U32, name="ew", align_bytes=64)
        xs = keep.tile([P, S], U8, name="xs", align_bytes=64)
        es = keep.tile([P, S], U8, name="es", align_bytes=64)
        inv_picked = keep.tile([P, S], F32, name="inv_picked", align_bytes=64)

        def interleave(copy, raw, name, tag=None):
            rounded = keep.tile([P, HALF * PACK], BF16, name=name, tag=tag or name, align_bytes=64)
            copy(
                out=rounded[:].rearrange("p (c i j) -> p c j i", i=4, j=PACK),
                in_=raw[:].rearrange("p j (c i) -> p c j i", i=4),
            )
            return rounded

        def negating_copy(out, in_):
            nc.scalar.activation(out=out, in_=in_, func=ACT.Copy, scale=-1.0)

        def signal_tiles(half):
            codes = keep.tile([P, 3 * HALF], U32, name="codes%d" % half, align_bytes=64)
            scales = keep.tile([P, 3 * HALF], U8, name="scales%d" % half, align_bytes=64)
            return codes, scales

        def quantize(signal, slot, rounded):
            codes, scales = signal
            cols = slice(slot * HALF, (slot + 1) * HALF)
            nc.vector.quantize_mx(out=codes[:, cols].bitcast(FP8X4), scales=scales[:, cols], in_=rounded[:])

        def product(acc, words, word_scales, atoms, signals, first_col, first):
            codes, scales = signals
            cols = slice(first_col, first_col + 2 * HALF)
            nc.tensor.matmul_mx(
                out=acc[:],
                lhsT=words[:, atoms].bitcast(FP8X4),
                lhsT_scale=word_scales[:, atoms],
                rhs=codes[:, cols].bitcast(FP8X4),
                rhs_scale=scales[:, cols],
                start=first,
                stop=not first,
            )

        atom_cols = [slice(a * P, (a + 1) * P) for a in range(N_ATOM_TILES)]

        nc.vector.tensor_copy(out=inv_picked[:], in_=inv_table[:].indirect(offsets[:]))
        inv_turned = bank(7, "inv_turned")
        for atoms in atom_cols:
            nc.tensor.transpose(inv_turned[:, atoms], inv_picked[:, atoms], identity[:])
        root_inv = keep.tile([P, N_ATOM_TILES], F32, name="root_inv", tag="after_squares")
        nc.vector.tensor_copy(out=xs[:], in_=xs_table[:].indirect(offsets[:]))
        inv_column = keep.tile([P, N_ATOM_TILES], F32, name="inv_column")
        nc.scalar.copy(out=inv_column[:], in_=inv_turned[:, 0 : S : P])
        nc.gpsimd.tensor_tensor(out=root_inv[:], in0=inv_column[:], in1=one_half[:], op=ALU.pow)
        nc.vector.tensor_copy(out=xw[:], in_=xw_table[:].bitcast(U32).indirect(offsets[:]))
        hr_rounded = [interleave(nc.scalar.copy, hr_raw[0], "hr_rounded0")]
        nc.vector.tensor_copy(out=es[:], in_=es_table[:].indirect(offsets[:]))
        negated = [interleave(negating_copy, hr_raw[0], "negated0")]
        hi_rounded = [interleave(nc.scalar.copy, hi_raw[0], "hi_rounded0")]
        signals = [signal_tiles(0)]
        for slot, rounded in ((0, hr_rounded[0]), (2, negated[0]), (1, hi_rounded[0])):
            quantize(signals[0], slot, rounded)

        for piece in range(2):
            nc.vector.tensor_copy(
                out=ew[:, piece * 256 : (piece + 1) * 256],
                in_=ew_table[:].bitcast(U32).indirect(offsets[:, piece * 16 : (piece + 1) * 16]),
            )
        hr_rounded.append(interleave(nc.vector.tensor_copy, hr_raw[1], "hr_rounded1", "hi_raw0"))
        negated.append(keep.tile([P, HALF * PACK], BF16, name="negated1", align_bytes=64))
        nc.vector.tensor_scalar(out=negated[1][:], in0=hr_rounded[1][:], scalar1=-1.0, scalar2=None, op0=ALU.mult)
        signals.append(signal_tiles(1))
        quantize(signals[1], 0, hr_rounded[1])
        quantize(signals[1], 2, negated[1])
        hi_rounded.append(interleave(nc.vector.tensor_copy, hi_raw[1], "hi_rounded1", "hi_raw0"))
        quantize(signals[1], 1, hi_rounded[1])

        product_banks = ((0, 1, 2, 3), (6, 7, 0, 1))
        match_banks = ((4, 5), (2, 3))

        def square(half, a, acc):
            name = "squares%d_%d" % (half, a)
            tag = name
            squares = keep.tile([P, 2 * HALF], F32, name=name, tag=tag, align_bytes=64)
            nc.scalar.activation(out=squares[:], in_=acc[:], func=ACT.Square, scale=root_inv[:, a : a + 1])
            return squares

        def turn(match, a, squares):
            for s in range(2):
                for part in range(2):
                    first_col = part * HALF + s * P
                    nc.tensor.matmul(
                        match[s][:, atom_cols[a]],
                        lhsT=squares[:, first_col : first_col + P],
                        rhs=identity[:],
                        is_transpose=True,
                        start=part == 0,
                        stop=part == 1,
                    )

        def add_and_turn(match, a, squares, engine, tag):
            summed = keep.tile([P, HALF], F32, name="summed_" + tag, tag=tag, align_bytes=64)
            engine.tensor_tensor(out=summed[:], in0=squares[:, 0:HALF], in1=squares[:, HALF : 2 * HALF], op=ALU.add)
            for s in range(2):
                nc.tensor.transpose(match[s][:, atom_cols[a]], summed[:, s * P : (s + 1) * P], identity[:])

        def find_slope(v, match):
            scratch = keep.tile([P, S], BF16, name="scratch", tag="scratch")
            top = keep.tile([P, 1], F32, name="top%d" % v)
            slope = keep.tile([P, 1], F32, name="slope%d" % v, tag="slope%d" % v)
            nc.vector.tensor_scalar(
                out=scratch[:], in0=match[:], scalar1=1.0 / SHARPNESS, scalar2=None,
                op0=ALU.mult, op1=ALU.max, accum_out=top[:],
            )
            nc.vector.reciprocal(out=slope[:], in_=top[:])
            return slope

        def softmax(v, match, slope):
            tag = ("after_squares", "slope0", "total2", "total3")[v]
            width = N_ATOM_TILES if v == 0 else 1
            totals = keep.tile([P, width], F32, name="total%d" % v, tag=tag)
            total = totals[:, width - 1 : width]
            norm = keep.tile([P, 1], F32, name="norm%d" % v)
            weights = keep.tile([P, S], F32, name="weights%d" % v)
            result = keep.tile([P, S], F32, name="result%d" % v)
            nc.scalar.activation(
                out=weights[:], in_=match[:], func=ACT.Exp, bias=shift[:], scale=slope[:], accum_out=total
            )
            if v == 0:
                nc.gpsimd.tensor_tensor(out=norm[:], in0=total, in1=minus_one[:], op=ALU.pow)
                nc.gpsimd.tensor_scalar(
                    out=result[:], in0=weights[:], scalar1=norm[:], scalar2=0.0, op0=ALU.mult, op1=ALU.add
                )
            else:
                nc.vector.reciprocal(out=norm[:], in_=total)
                cols = slice(0, 256 if v == 3 else 512)
                nc.vector.tensor_scalar(
                    out=result[:, cols], in0=weights[:, cols], scalar1=norm[:], scalar2=None, op0=ALU.mult
                )
                nc.sync.dma_start(out=out[v * P : (v + 1) * P, cols], in_=result[:, cols])
                if v == 3:
                    cols = slice(256, 512)
                    nc.scalar.activation(out=result[:, cols], in_=weights[:, cols], func=ACT.Copy, scale=norm[:])
                    nc.scalar.dma_start(out=out[v * P : (v + 1) * P, cols], in_=result[:, cols])
                return
            nc.sync.dma_start(out=out[v * P : (v + 1) * P, :], in_=result[:])

        accs = [bank(b, "acc0_%d" % a) for a, b in enumerate(product_banks[0])]
        for a in range(N_ATOM_TILES):
            product(accs[a], xw, xs, atom_cols[a], signals[0], 0, True)
        for a in range(N_ATOM_TILES):
            product(accs[a], ew, es, atom_cols[a], signals[0], HALF, False)
        squares0 = [square(0, a, accs[a]) for a in range(N_ATOM_TILES)]

        match0 = [bank(b, "match0_%d" % s) for s, b in enumerate(match_banks[0])]
        for a in range(N_ATOM_TILES - 1):
            turn(match0, a, squares0[a])
        squares1 = []
        for a in range(N_ATOM_TILES):
            acc = bank(product_banks[1][a], "acc1_%d" % a)
            product(acc, xw, xs, atom_cols[a], signals[1], 0, True)
            product(acc, ew, es, atom_cols[a], signals[1], HALF, False)
            squares1.append(square(1, a, acc))
            if a == 0:
                add_and_turn(match0, 3, squares0[3], nc.vector, "hi_raw0")
        slopes = [find_slope(s, match0[s]) for s in range(2)]
        match1 = [bank(b, "match1_%d" % s) for s, b in enumerate(match_banks[1])]
        for a in range(N_ATOM_TILES - 1):
            add_and_turn(match1, a, squares1[a], nc.gpsimd if a == 0 else nc.vector, "sum%d" % a)
        turn(match1, 3, squares1[3])
        slopes.extend(find_slope(2 + s, match1[s]) for s in range(2))
        for v, match in enumerate(match0 + match1):
            softmax(v, match, slopes[v])
